import numpy as np, ml_dtypes
CORES = [0,1,2,3]
N = 4
ROOT = 3
def setup_inputs(rng):
    return {"x": rng.standard_normal((N, 128, 256), dtype=np.float32).astype(ml_dtypes.bfloat16)}
def reference(x):
    y = np.full(x.shape, np.nan, x.dtype)
    y[ROOT] = x.sum(axis=0, dtype=np.float64).astype(x.dtype)
    return {"y": y}

from concourse.bass import DstId, RemoteDMATransfer
from concourse.mybir import AluOpType

SCRATCH = {
    "stage": ("dram", [128, 256], "bfloat16"),
    "land0": ("dram", [128, 256], "bfloat16"),
    "land1": ("dram", [128, 256], "bfloat16"),
    "part": ("dram", [128, 256], "bfloat16"),
}
SEMAPHORES = ["loaded", "arrived", "sent", "stored"]

ALL16 = 0xFFFF


def rank_program(g, core, T, topo):
    rank = T.rank_of(core)
    if rank is None:
        return
    root = T.cores[3]
    folder = T.cores[2]

    if core == root:
        g.sync.dma_start(T.y[:], T.x[:]).then_inc(T.sem.loaded, 16)
        g.wait_ge(T.sem.loaded, 16)
        g.wait_ge(T.sem.arrived, 16)
        g.dma_start(T.y[:], T.part[:], accum_op=AluOpType.add, max_dma_last_dim=4096).then_inc(T.sem.stored, 16)
        g.wait_ge(T.sem.stored, 16)
        return

    g.sync.dma_start(T.stage[:], T.x[:]).then_inc(T.sem.loaded, 16)
    g.wait_ge(T.sem.loaded, 16)

    if core == folder:
        rid, pid, _se = topo.addr(root)
        g.wait_ge(T.sem.arrived, 32)
        g.remote_dma_fused(
            [RemoteDMATransfer(dst_ids=[DstId(rid=rid, pnc=pid)], dma_engine_mask=ALL16, remote_sem=T.sem.arrived,
                               srcs=[T.stage[:], T.land0[:], T.land1[:]], dsts=[T.part[:]], alu_op=1)],
            local_sem=T.sem.sent)
    else:
        rid, pid, _se = topo.addr(folder)
        g.remote_dma(out_ap=T["land%d" % rank][:], in_ap=T.stage[:], remote_sem=T.sem.arrived,
                     local_sem=T.sem.sent, pid=pid, routing_id=rid, dma_engine_mask=ALL16)
    g.wait_ge(T.sem.sent, 16)
